import numpy as np
import ml_dtypes


def mxq(x, axis, fmt="e4m3"):
    dtype, down = {"e4m3": (ml_dtypes.float8_e4m3fn, 7), "e5m2": (ml_dtypes.float8_e5m2, 14)}[fmt]
    v = np.moveaxis(np.asarray(x, np.float32).astype(ml_dtypes.bfloat16).astype(np.float64), axis, -1)
    blocks = v.reshape(v.shape[:-1] + (-1, 32))
    amax = np.abs(blocks).max(-1, keepdims=True)
    byte = np.maximum(np.where(amax > 0, np.frexp(amax)[1] - 1 + 127, 0) - down, 1)
    scale = np.exp2(byte - 127.0)
    codes = (blocks / scale).astype(np.float32).astype(dtype).astype(np.float64)
    return np.moveaxis((codes * scale).reshape(v.shape), -1, axis)


WIDE = False


def mx_kscale(k):
    if not WIDE:
        return np.ones(k)
    levels = np.array([10, -10, 5, -5, 0])
    if k % 512:
        return np.exp2(np.random.permutation(np.resize(levels, k // 32))).repeat(32)
    a = np.empty((k // 512, 16))
    for p in range(k // 512):
        a[p, :8] = np.random.permutation(np.resize(levels, 8))
        for g in range(8):
            far = levels[np.abs(levels - a[p, g]) >= 10]
            a[p, g + 8] = far[np.random.randint(len(far))]
    return np.exp2(a.ravel()).repeat(32)


def f64(x):
    return np.asarray(x).astype(np.float64)


def striped(idx):
    return np.tile(idx.reshape(-1, 16).T, (8, 1)).astype(np.uint16)


def unstriped(offs):
    return offs[:16].T.reshape(-1).astype(np.int64)


def striped8(idx):
    return np.concatenate([x.reshape(-1, 16).T for x in idx]).astype(np.uint16)


def runs(offs, k):
    lists = np.stack([offs[16 * r : 16 * r + 16].T.reshape(-1) for r in range(8)]).astype(np.int64)
    return lists[np.arange(k) % 512 // 64]


def pack_weight(w):
    k, n = w.shape
    w = f64(np.asarray(w, np.float32).astype(ml_dtypes.bfloat16)).reshape(k // 32, 32, n)
    amax = np.abs(w).max(1)
    byte = np.clip(np.where(amax > 0, np.frexp(amax)[1] - 1 + 127 - 7, 1), 1, 254)
    scaled = (w * np.exp2(127.0 - byte)[:, None, :]).reshape(k, n).astype(np.float32)
    words = np.ascontiguousarray(scaled.reshape(k // 512, 128, 4, n).transpose(0, 1, 3, 2)).astype(ml_dtypes.float8_e4m3fn).view(np.uint8)
    return words, np.ascontiguousarray(byte.astype(np.uint8).reshape(k // 512, 16, n))


def unpack_weight(words, scales):
    g, p, n, _ = words.shape
    vals = np.ascontiguousarray(words).view(ml_dtypes.float8_e4m3fn).astype(np.float64) * np.repeat(np.exp2(scales.astype(np.float64) - 127.0), 8, axis=1)[..., None]
    return vals.transpose(0, 1, 3, 2).reshape(g * 512, n)


def sigmoid(v):
    return 1.0 / (1.0 + np.exp(-np.maximum(v, -700.0)))


K, T, S, G, H = 512, 2048, 512, 2048, 512


def setup_inputs():
    n = np.random.standard_normal
    s = mx_kscale(K)[:, None]
    packed_xT = pack_weight(n((K, T)) * s)
    packed_dT = pack_weight(n((K, G)) / s)
    return {
        "x_words": packed_xT[0],
        "x_scales": packed_xT[1],
        "d_words": packed_dT[0],
        "d_scales": packed_dT[1],
        "gs": (np.random.uniform(0.5, 1.5, (K, 1)) * s).astype(np.float32),
        "offs": striped(np.random.permutation(T)[:S]),
        "k1": striped8(np.random.randint(0, G, (8, H))),
        "n1": striped8(np.stack([np.random.permutation(S) for _ in range(8)])),
        "n2": striped8(np.stack([np.random.permutation(S) for _ in range(8)])),
        "k2": striped8(np.random.randint(0, G, (8, H))),
    }


def reference(x_words, x_scales, d_words, d_scales, gs, offs, k1, n1, n2, k2):
    d_k2 = unpack_weight(d_words, d_scales)[np.arange(K)[:, None], runs(k2, K)]
    d_k1 = unpack_weight(d_words, d_scales)[np.arange(K)[:, None], runs(k1, K)]
    xq = unpack_weight(x_words, x_scales)[:, unstriped(offs)]
    h = 0.0625 * (d_k1.T @ xq)
    z = f64(gs) * ((h[np.arange(H)[:, None], runs(n1, H)]) * (sigmoid(h[np.arange(H)[:, None], runs(n2, H)])))
    return 0.0625 * ((d_k2.T @ mxq(z, 0, "e4m3")))

@@ -1,0 +1,170 @@
+from contextlib import ExitStack
+
+import concourse.mybir as mybir
+
+F32 = mybir.dt.float32
+BF16 = mybir.dt.bfloat16
+I32 = mybir.dt.int32
+U32 = mybir.dt.uint32
+U16 = mybir.dt.uint16
+U8 = mybir.dt.uint8
+FP8X4 = mybir.dt.float8_e4m3fn_x4
+ACT = mybir.ActivationFunctionType
+MULT = mybir.AluOpType.mult
+ADD = mybir.AluOpType.add
+
+P = 128
+PACK = 4
+TABLE = 2048
+S = 512
+SIXTEENTH = 0.0625
+CHUNKS = [128,128,128,128]
+GAIN_ON_SCALAR = 2
+FLOPS = 2 * 2 * 512 * 512 * 512
+
+
+def tile_picked_pqgate_none_p_kernel(
+    tc, x_words, x_scales, d_words, d_scales, gs, offs, k1, n1, n2, k2, out
+):
+    nc = tc.nc
+    with ExitStack() as ctx:
+        lists = ctx.enter_context(tc.tile_pool(name="lists", bufs=1))
+        keep = ctx.enter_context(tc.tile_pool(name="keep", bufs=1))
+        psum = ctx.enter_context(tc.psum_pool(name="psum", bufs=1))
+
+        def load_list(src, name):
+            t = lists.tile([P, S // 16], U16, name=name)
+            nc.sync.dma_start(t[:], src)
+            return t
+
+        def words_view(src):
+            return src[0].rearrange("p c r -> p (c r)").bitcast(I32)
+
+        ds_win = keep.tile([P, TABLE], U8, name="ds_win")
+        xs_win = keep.tile([P, TABLE], U8, name="xs_win")
+        warm = keep.tile([P, 1], F32, name="warm")
+        warm_out = keep.tile([P, 1], F32, name="warm_out")
+        nc.vector.memset(warm[:], 0.0)
+        nc.scalar.activation(warm_out[:], warm[:], ACT.Sigmoid)
+
+        def load_scales(win, src):
+            rows = src[0].bitcast(I32).unsqueeze(1).to_broadcast([16, 8, TABLE // 4])
+            nc.sync.dma_start(win[:].bitcast(I32), rows)
+
+        k1_t = load_list(k1, "k1_t")
+        load_scales(ds_win, d_scales)
+        offs_t = load_list(offs, "offs_t")
+        load_scales(xs_win, x_scales)
+        dw_win = keep.tile([P, TABLE], I32, name="dw_win")
+        xw_win = keep.tile([P, TABLE], I32, name="xw_win")
+        nc.sync.dma_start(dw_win[:], words_view(d_words))
+        nc.sync.dma_start(xw_win[:], words_view(x_words))
+        k2_t = load_list(k2, "k2_t")
+        n2_t = load_list(n2, "n2_t")
+        n1_t = load_list(n1, "n1_t")
+        gain = keep.tile([P, PACK], F32, name="gain")
+        nc.gpsimd.dma_start(gain[:], gs.rearrange("(p t) o -> p (t o)", t=PACK))
+        gain16 = keep.tile([P, PACK], F32, name="gain16")
+        nc.gpsimd.tensor_scalar(gain16[:], gain[:], SIXTEENTH, 0.0, MULT, ADD)
+
+        def gather(win, lst, dtype, name):
+            t = keep.tile([P, S], dtype, name=name, align_bytes=64)
+            nc.vector.tensor_copy(t[:], win.indirect(lst[:]))
+            return t
+
+        def place_rows(plane, queue):
+            for e in range(1, 4):
+                queue.dma_start(plane[e:P:32, :].bitcast(I32), plane[8 * e : P : 32, :].bitcast(I32))
+
+        w1s_raw = gather(ds_win[:], k1_t, U8, "w1s_raw")
+        xs_raw = gather(xs_win[:], offs_t, U8, "xs_raw")
+        plane1 = keep.tile([P, 2 * S], U8, name="plane1", align_bytes=64)
+        nc.vector.tensor_copy(
+            plane1[:, 0:S].rearrange("p (t m) -> p t m", t=PACK), w1s_raw[:].rearrange("p (m t) -> p t m", t=PACK)
+        )
+        nc.vector.tensor_copy(plane1[:, S : 2 * S].bitcast(I32), xs_raw[:].bitcast(I32))
+        place_rows(plane1, nc.scalar)
+
+        w1_raw = gather(dw_win[:].bitcast(U32), k1_t, U32, "w1_raw")
+        w1 = keep.tile([P, S], U32, name="w1", align_bytes=64)
+        nc.vector.tensor_copy(
+            w1[:].rearrange("p (t m) -> p t m", t=PACK), w1_raw[:].rearrange("p (m t) -> p t m", t=PACK)
+        )
+        xq = gather(xw_win[:].bitcast(U32), offs_t, U32, "xq")
+
+        h_ps = [psum.tile([P, S], F32, name="h_ps%d" % t) for t in range(PACK)]
+        for t in range(PACK):
+            cols = slice(t * P, (t + 1) * P)
+            nc.tensor.matmul_mx(
+                out=h_ps[t][:], lhsT=w1[:, cols].bitcast(FP8X4), lhsT_scale=plane1[:, cols],
+                rhs=xq[:].bitcast(FP8X4), rhs_scale=plane1[:, S : 2 * S], start=True, stop=True,
+            )
+
+        w2s_raw = gather(ds_win[:], k2_t, U8, "w2s_raw")
+        plane2 = keep.tile([P, S], U8, name="plane2", align_bytes=64)
+        nc.vector.tensor_copy(plane2[:].bitcast(I32), w2s_raw[:].bitcast(I32))
+        place_rows(plane2, nc.sync)
+        w2 = gather(dw_win[:].bitcast(U32), k2_t, U32, "w2")
+
+        h = [keep.tile([P, S], F32, name="h%d" % t) for t in range(PACK)]
+        hg = [keep.tile([P, S], F32, name="hg%d" % t) for t in range(PACK)]
+
+        def leave_psum(t):
+            nc.scalar.activation(h[t][:], h_ps[t][:], ACT.Copy, scale=SIXTEENTH)
+            if t < GAIN_ON_SCALAR:
+                nc.scalar.activation(hg[t][:], h_ps[t][:], ACT.Copy, scale=gain16[:, t : t + 1])
+            else:
+                nc.vector.tensor_scalar(hg[t][:], h[t][:], gain[:, t : t + 1], None, MULT)
+
+        starts = [sum(CHUNKS[:c]) for c in range(len(CHUNKS))]
+        z = [keep.tile([P, PACK, w], F32, name="z%d" % c) for c, w in enumerate(CHUNKS)]
+        zb = [keep.tile([P, w, PACK], BF16, name="zb%d" % c, align_bytes=64) for c, w in enumerate(CHUNKS)]
+
+        def gate(c, t):
+            w = CHUNKS[c]
+            lc = slice(starts[c] // 16, (starts[c] + w) // 16)
+            sg = keep.tile([P, w], F32, name="sg%d_%d" % (c, t))
+            nc.scalar.activation(sg[:], h[t][:].indirect(n2_t[:, lc]), ACT.Sigmoid)
+            nc.vector.tensor_tensor(z[c][:, t, :], hg[t][:].indirect(n1_t[:, lc]), sg[:], MULT)
+
+        def weave(c):
+            nc.vector.tensor_copy(
+                zb[c][:].rearrange("p (g i) t -> p g t i", i=4), z[c][:].rearrange("p t (g i) -> p g t i", i=4)
+            )
+
+        out_v = out.rearrange("(m p) j -> p m j", p=P)
+
+        def finish(c):
+            w = CHUNKS[c]
+            zq = keep.tile([P, w], U32, name="zq%d" % c, align_bytes=64)
+            zs = keep.tile([P, w], U8, name="zs%d" % c, align_bytes=64)
+            nc.vector.quantize_mx(out=zq[:].bitcast(FP8X4), scales=zs[:], in_=zb[c][:].rearrange("p j t -> p (j t)"))
+            last = c == len(CHUNKS) - 1
+            per_bank = 2 if last else S // w
+            for m0 in range(0, PACK, per_bank):
+                o_ps = psum.tile([P, per_bank, w], F32, name="o_ps", tag="o_ps", bufs=4)
+                for m in range(m0, m0 + per_bank):
+                    cols = slice(m * P, (m + 1) * P)
+                    nc.tensor.matmul_mx(
+                        out=o_ps[:, m - m0, :], lhsT=w2[:, cols].bitcast(FP8X4), lhsT_scale=plane2[:, cols],
+                        rhs=zq[:].bitcast(FP8X4), rhs_scale=zs[:], start=True, stop=True,
+                    )
+                o_sb = keep.tile([P, per_bank, w], F32, name="o_sb%d_%d" % (c, m0))
+                if last and m0 > 0:
+                    nc.vector.tensor_scalar(o_sb[:], o_ps[:], SIXTEENTH, None, MULT)
+                else:
+                    nc.scalar.activation(o_sb[:], o_ps[:], ACT.Copy, scale=SIXTEENTH)
+                nc.sync.dma_start(out_v[:, m0 : m0 + per_bank, starts[c] : starts[c] + w], o_sb[:])
+
+        for t in range(PACK):
+            leave_psum(t)
+            gate(0, t)
+        for c in range(1, len(CHUNKS)):
+            gate(c, 0)
+            weave(c - 1)
+            gate(c, 1)
+            finish(c - 1)
+            gate(c, 2)
+            gate(c, 3)
+        weave(len(CHUNKS) - 1)
+        finish(len(CHUNKS) - 1)

@@ -18,8 +18,9 @@ PACK = 4
 TABLE = 2048
 S = 512
 SIXTEENTH = 0.0625
-CHUNKS = [128,128,128,128]
-GAIN_ON_SCALAR = 2
+CHUNKS = [256,128,128]
+WEAVE_ON_SCALAR = 0
+RING = 4
 FLOPS = 2 * 2 * 512 * 512 * 512
 
 
@@ -51,8 +52,8 @@ def tile_picked_pqgate_none_p_kernel(
             rows = src[0].bitcast(I32).unsqueeze(1).to_broadcast([16, 8, TABLE // 4])
             nc.sync.dma_start(win[:].bitcast(I32), rows)
 
-        k1_t = load_list(k1, "k1_t")
         load_scales(ds_win, d_scales)
+        k1_t = load_list(k1, "k1_t")
         offs_t = load_list(offs, "offs_t")
         load_scales(xs_win, x_scales)
         dw_win = keep.tile([P, TABLE], I32, name="dw_win")
@@ -64,8 +65,6 @@ def tile_picked_pqgate_none_p_kernel(
         n1_t = load_list(n1, "n1_t")
         gain = keep.tile([P, PACK], F32, name="gain")
         nc.gpsimd.dma_start(gain[:], gs.rearrange("(p t) o -> p (t o)", t=PACK))
-        gain16 = keep.tile([P, PACK], F32, name="gain16")
-        nc.gpsimd.tensor_scalar(gain16[:], gain[:], SIXTEENTH, 0.0, MULT, ADD)
 
         def gather(win, lst, dtype, name):
             t = keep.tile([P, S], dtype, name=name, align_bytes=64)
@@ -80,7 +79,8 @@ def tile_picked_pqgate_none_p_kernel(
         xs_raw = gather(xs_win[:], offs_t, U8, "xs_raw")
         plane1 = keep.tile([P, 2 * S], U8, name="plane1", align_bytes=64)
         nc.vector.tensor_copy(
-            plane1[:, 0:S].rearrange("p (t m) -> p t m", t=PACK), w1s_raw[:].rearrange("p (m t) -> p t m", t=PACK)
+            plane1[:, 0:S].rearrange("p (t g i) -> p g t i", t=PACK, i=16),
+            w1s_raw[:].rearrange("p (g i t) -> p g t i", t=PACK, i=16),
         )
         nc.vector.tensor_copy(plane1[:, S : 2 * S].bitcast(I32), xs_raw[:].bitcast(I32))
         place_rows(plane1, nc.scalar)
@@ -88,7 +88,8 @@ def tile_picked_pqgate_none_p_kernel(
         w1_raw = gather(dw_win[:].bitcast(U32), k1_t, U32, "w1_raw")
         w1 = keep.tile([P, S], U32, name="w1", align_bytes=64)
         nc.vector.tensor_copy(
-            w1[:].rearrange("p (t m) -> p t m", t=PACK), w1_raw[:].rearrange("p (m t) -> p t m", t=PACK)
+            w1[:].rearrange("p (t g i) -> p g t i", t=PACK, i=4),
+            w1_raw[:].rearrange("p (g i t) -> p g t i", t=PACK, i=4),
         )
         xq = gather(xw_win[:].bitcast(U32), offs_t, U32, "xq")
 
@@ -111,26 +112,28 @@ def tile_picked_pqgate_none_p_kernel(
 
         def leave_psum(t):
             nc.scalar.activation(h[t][:], h_ps[t][:], ACT.Copy, scale=SIXTEENTH)
-            if t < GAIN_ON_SCALAR:
-                nc.scalar.activation(hg[t][:], h_ps[t][:], ACT.Copy, scale=gain16[:, t : t + 1])
-            else:
-                nc.vector.tensor_scalar(hg[t][:], h[t][:], gain[:, t : t + 1], None, MULT)
+            nc.vector.tensor_scalar(hg[t][:], h[t][:], gain[:, t : t + 1], None, MULT)
 
         starts = [sum(CHUNKS[:c]) for c in range(len(CHUNKS))]
         z = [keep.tile([P, PACK, w], F32, name="z%d" % c) for c, w in enumerate(CHUNKS)]
         zb = [keep.tile([P, w, PACK], BF16, name="zb%d" % c, align_bytes=64) for c, w in enumerate(CHUNKS)]
 
+        sg_ring = [keep.tile([P, max(CHUNKS)], F32, name="sg%d" % i) for i in range(RING)]
+
         def gate(c, t):
             w = CHUNKS[c]
             lc = slice(starts[c] // 16, (starts[c] + w) // 16)
-            sg = keep.tile([P, w], F32, name="sg%d_%d" % (c, t))
-            nc.scalar.activation(sg[:], h[t][:].indirect(n2_t[:, lc]), ACT.Sigmoid)
-            nc.vector.tensor_tensor(z[c][:, t, :], hg[t][:].indirect(n1_t[:, lc]), sg[:], MULT)
+            sg = sg_ring[(PACK * c + t) % RING][:, 0:w]
+            nc.scalar.activation(sg, h[t][:].indirect(n2_t[:, lc]), ACT.Sigmoid)
+            nc.vector.tensor_tensor(z[c][:, t, :], hg[t][:].indirect(n1_t[:, lc]), sg, MULT)
 
         def weave(c):
-            nc.vector.tensor_copy(
-                zb[c][:].rearrange("p (g i) t -> p g t i", i=4), z[c][:].rearrange("p t (g i) -> p g t i", i=4)
-            )
+            dst = zb[c][:].rearrange("p (g i) t -> p g t i", i=4)
+            src = z[c][:].rearrange("p t (g i) -> p g t i", i=4)
+            if c < WEAVE_ON_SCALAR:
+                nc.scalar.copy(dst, src)
+            else:
+                nc.vector.tensor_copy(dst, src)
 
         out_v = out.rearrange("(m p) j -> p m j", p=P)
 

@@ -19,8 +19,8 @@ TABLE = 2048
 S = 512
 SIXTEENTH = 0.0625
 CHUNKS = [256,128,128]
-WEAVE_ON_SCALAR = 0
-RING = 4
+WEAVE_ON_SCALAR = 1
+RING = 6
 FLOPS = 2 * 2 * 512 * 512 * 512
 
 
@@ -45,6 +45,8 @@ def tile_picked_pqgate_none_p_kernel(
         xs_win = keep.tile([P, TABLE], U8, name="xs_win")
         warm = keep.tile([P, 1], F32, name="warm")
         warm_out = keep.tile([P, 1], F32, name="warm_out")
+        nc.gpsimd.memset(xs_win[:, 0 : TABLE // 2].bitcast(I32), 0)
+        nc.vector.memset(xs_win[:, TABLE // 2 : TABLE].bitcast(I32), 0)
         nc.vector.memset(warm[:], 0.0)
         nc.scalar.activation(warm_out[:], warm[:], ACT.Sigmoid)
 
@@ -55,14 +57,14 @@ def tile_picked_pqgate_none_p_kernel(
         load_scales(ds_win, d_scales)
         k1_t = load_list(k1, "k1_t")
         offs_t = load_list(offs, "offs_t")
-        load_scales(xs_win, x_scales)
+        n2_t = load_list(n2, "n2_t")
+        n1_t = load_list(n1, "n1_t")
+        nc.sync.dma_start(xs_win[0:P:8, :].bitcast(I32), x_scales[0].bitcast(I32))
         dw_win = keep.tile([P, TABLE], I32, name="dw_win")
         xw_win = keep.tile([P, TABLE], I32, name="xw_win")
         nc.sync.dma_start(dw_win[:], words_view(d_words))
         nc.sync.dma_start(xw_win[:], words_view(x_words))
         k2_t = load_list(k2, "k2_t")
-        n2_t = load_list(n2, "n2_t")
-        n1_t = load_list(n1, "n1_t")
         gain = keep.tile([P, PACK], F32, name="gain")
         nc.gpsimd.dma_start(gain[:], gs.rearrange("(p t) o -> p (t o)", t=PACK))
 
@@ -91,14 +93,18 @@ def tile_picked_pqgate_none_p_kernel(
             w1[:].rearrange("p (t g i) -> p g t i", t=PACK, i=4),
             w1_raw[:].rearrange("p (g i t) -> p g t i", t=PACK, i=4),
         )
-        xq = gather(xw_win[:].bitcast(U32), offs_t, U32, "xq")
-
         h_ps = [psum.tile([P, S], F32, name="h_ps%d" % t) for t in range(PACK)]
-        for t in range(PACK):
+        half = S // 2
+        xq = keep.tile([P, S], U32, name="xq", align_bytes=64)
+        for lo in (0, half):
+            nc.vector.tensor_copy(
+                xq[:, lo : lo + half], xw_win[:].bitcast(U32).indirect(offs_t[:, lo // 16 : (lo + half) // 16])
+            )
+        for t, lo, hi in ((0, 0, half), (1, 0, half), (0, half, S), (1, half, S), (2, 0, S), (3, 0, S)):
             cols = slice(t * P, (t + 1) * P)
             nc.tensor.matmul_mx(
-                out=h_ps[t][:], lhsT=w1[:, cols].bitcast(FP8X4), lhsT_scale=plane1[:, cols],
-                rhs=xq[:].bitcast(FP8X4), rhs_scale=plane1[:, S : 2 * S], start=True, stop=True,
+                out=h_ps[t][:, lo:hi], lhsT=w1[:, cols].bitcast(FP8X4), lhsT_scale=plane1[:, cols],
+                rhs=xq[:, lo:hi].bitcast(FP8X4), rhs_scale=plane1[:, S + lo : S + hi], start=True, stop=True,
             )
 
         w2s_raw = gather(ds_win[:], k2_t, U8, "w2s_raw")
@@ -115,7 +121,7 @@ def tile_picked_pqgate_none_p_kernel(
             nc.vector.tensor_scalar(hg[t][:], h[t][:], gain[:, t : t + 1], None, MULT)
 
         starts = [sum(CHUNKS[:c]) for c in range(len(CHUNKS))]
-        z = [keep.tile([P, PACK, w], F32, name="z%d" % c) for c, w in enumerate(CHUNKS)]
+        z = [keep.tile([P, PACK, w], F32, name="z%d" % c, tag="z%d" % c) for c, w in enumerate(CHUNKS)]
         zb = [keep.tile([P, w, PACK], BF16, name="zb%d" % c, align_bytes=64) for c, w in enumerate(CHUNKS)]
 
         sg_ring = [keep.tile([P, max(CHUNKS)], F32, name="sg%d" % i) for i in range(RING)]
@@ -130,14 +136,16 @@ def tile_picked_pqgate_none_p_kernel(
         def weave(c):
             dst = zb[c][:].rearrange("p (g i) t -> p g t i", i=4)
             src = z[c][:].rearrange("p t (g i) -> p g t i", i=4)
-            if c < WEAVE_ON_SCALAR:
+            if c == WEAVE_ON_SCALAR:
                 nc.scalar.copy(dst, src)
             else:
                 nc.vector.tensor_copy(dst, src)
 
         out_v = out.rearrange("(m p) j -> p m j", p=P)
 
-        def finish(c):
+        banks = {}
+
+        def multiply(c):
             w = CHUNKS[c]
             zq = keep.tile([P, w], U32, name="zq%d" % c, align_bytes=64)
             zs = keep.tile([P, w], U8, name="zs%d" % c, align_bytes=64)
@@ -152,7 +160,16 @@ def tile_picked_pqgate_none_p_kernel(
                         out=o_ps[:, m - m0, :], lhsT=w2[:, cols].bitcast(FP8X4), lhsT_scale=plane2[:, cols],
                         rhs=zq[:].bitcast(FP8X4), rhs_scale=zs[:], start=True, stop=True,
                     )
-                o_sb = keep.tile([P, per_bank, w], F32, name="o_sb%d_%d" % (c, m0))
+                banks[(c, m0)] = o_ps
+
+        def leave(c):
+            w = CHUNKS[c]
+            last = c == len(CHUNKS) - 1
+            per_bank = 2 if last else S // w
+            for m0 in range(0, PACK, per_bank):
+                o_ps = banks[(c, m0)]
+                tag = "z1" if (c, m0) == (0, 0) else "o_sb%d_%d" % (c, m0)
+                o_sb = keep.tile([P, per_bank, w], F32, name="o_sb%d_%d" % (c, m0), tag=tag)
                 if last and m0 > 0:
                     nc.vector.tensor_scalar(o_sb[:], o_ps[:], SIXTEENTH, None, MULT)
                 else:
@@ -162,12 +179,20 @@ def tile_picked_pqgate_none_p_kernel(
         for t in range(PACK):
             leave_psum(t)
             gate(0, t)
-        for c in range(1, len(CHUNKS)):
-            gate(c, 0)
-            weave(c - 1)
-            gate(c, 1)
-            finish(c - 1)
-            gate(c, 2)
-            gate(c, 3)
-        weave(len(CHUNKS) - 1)
-        finish(len(CHUNKS) - 1)
+        gate(1, 0)
+        weave(0)
+        gate(1, 1)
+        multiply(0)
+        gate(1, 2)
+        gate(1, 3)
+        weave(1)
+        leave(0)
+        gate(2, 0)
+        gate(2, 1)
+        multiply(1)
+        leave(1)
+        gate(2, 2)
+        gate(2, 3)
+        weave(2)
+        multiply(2)
+        leave(2)

from contextlib import ExitStack

import concourse.mybir as mybir

F32 = mybir.dt.float32
BF16 = mybir.dt.bfloat16
I32 = mybir.dt.int32
U32 = mybir.dt.uint32
U16 = mybir.dt.uint16
U8 = mybir.dt.uint8
FP8X4 = mybir.dt.float8_e4m3fn_x4
ACT = mybir.ActivationFunctionType
MULT = mybir.AluOpType.mult
ADD = mybir.AluOpType.add

P = 128
PACK = 4
TABLE = 2048
S = 512
SIXTEENTH = 0.0625
CHUNKS = [256,128,128]
WEAVE_ON_SCALAR = 1
RING = 6
FLOPS = 2 * 2 * 512 * 512 * 512


def tile_picked_pqgate_none_p_kernel(
    tc, x_words, x_scales, d_words, d_scales, gs, offs, k1, n1, n2, k2, out
):
    nc = tc.nc
    with ExitStack() as ctx:
        lists = ctx.enter_context(tc.tile_pool(name="lists", bufs=1))
        keep = ctx.enter_context(tc.tile_pool(name="keep", bufs=1))
        psum = ctx.enter_context(tc.psum_pool(name="psum", bufs=1))

        def load_list(src, name):
            t = lists.tile([P, S // 16], U16, name=name)
            nc.sync.dma_start(t[:], src)
            return t

        def words_view(src):
            return src[0].rearrange("p c r -> p (c r)").bitcast(I32)

        ds_win = keep.tile([P, TABLE], U8, name="ds_win")
        xs_win = keep.tile([P, TABLE], U8, name="xs_win")
        warm = keep.tile([P, 1], F32, name="warm")
        warm_out = keep.tile([P, 1], F32, name="warm_out")
        nc.gpsimd.memset(xs_win[:, 0 : TABLE // 2].bitcast(I32), 0)
        nc.vector.memset(xs_win[:, TABLE // 2 : TABLE].bitcast(I32), 0)
        nc.vector.memset(warm[:], 0.0)
        nc.scalar.activation(warm_out[:], warm[:], ACT.Sigmoid)

        def load_scales(win, src):
            rows = src[0].bitcast(I32).unsqueeze(1).to_broadcast([16, 8, TABLE // 4])
            nc.sync.dma_start(win[:].bitcast(I32), rows)

        load_scales(ds_win, d_scales)
        k1_t = load_list(k1, "k1_t")
        offs_t = load_list(offs, "offs_t")
        n2_t = load_list(n2, "n2_t")
        n1_t = load_list(n1, "n1_t")
        nc.sync.dma_start(xs_win[0:P:8, :].bitcast(I32), x_scales[0].bitcast(I32))
        dw_win = keep.tile([P, TABLE], I32, name="dw_win")
        xw_win = keep.tile([P, TABLE], I32, name="xw_win")
        nc.sync.dma_start(dw_win[:], words_view(d_words))
        nc.sync.dma_start(xw_win[:], words_view(x_words))
        k2_t = load_list(k2, "k2_t")
        gain = keep.tile([P, PACK], F32, name="gain")
        nc.gpsimd.dma_start(gain[:], gs.rearrange("(p t) o -> p (t o)", t=PACK))

        def gather(win, lst, dtype, name):
            t = keep.tile([P, S], dtype, name=name, align_bytes=64)
            nc.vector.tensor_copy(t[:], win.indirect(lst[:]))
            return t

        def place_rows(plane, queue):
            for e in range(1, 4):
                queue.dma_start(plane[e:P:32, :].bitcast(I32), plane[8 * e : P : 32, :].bitcast(I32))

        w1s_raw = gather(ds_win[:], k1_t, U8, "w1s_raw")
        xs_raw = gather(xs_win[:], offs_t, U8, "xs_raw")
        plane1 = keep.tile([P, 2 * S], U8, name="plane1", align_bytes=64)
        nc.vector.tensor_copy(
            plane1[:, 0:S].rearrange("p (t g i) -> p g t i", t=PACK, i=16),
            w1s_raw[:].rearrange("p (g i t) -> p g t i", t=PACK, i=16),
        )
        nc.vector.tensor_copy(plane1[:, S : 2 * S].bitcast(I32), xs_raw[:].bitcast(I32))
        place_rows(plane1, nc.scalar)

        w1_raw = gather(dw_win[:].bitcast(U32), k1_t, U32, "w1_raw")
        w1 = keep.tile([P, S], U32, name="w1", align_bytes=64)
        nc.vector.tensor_copy(
            w1[:].rearrange("p (t g i) -> p g t i", t=PACK, i=4),
            w1_raw[:].rearrange("p (g i t) -> p g t i", t=PACK, i=4),
        )
        h_ps = [psum.tile([P, S], F32, name="h_ps%d" % t) for t in range(PACK)]
        half = S // 2
        xq = keep.tile([P, S], U32, name="xq", align_bytes=64)
        for lo in (0, half):
            nc.vector.tensor_copy(
                xq[:, lo : lo + half], xw_win[:].bitcast(U32).indirect(offs_t[:, lo // 16 : (lo + half) // 16])
            )
        for t, lo, hi in ((0, 0, half), (1, 0, half), (0, half, S), (1, half, S), (2, 0, S), (3, 0, S)):
            cols = slice(t * P, (t + 1) * P)
            nc.tensor.matmul_mx(
                out=h_ps[t][:, lo:hi], lhsT=w1[:, cols].bitcast(FP8X4), lhsT_scale=plane1[:, cols],
                rhs=xq[:, lo:hi].bitcast(FP8X4), rhs_scale=plane1[:, S + lo : S + hi], start=True, stop=True,
            )

        w2s_raw = gather(ds_win[:], k2_t, U8, "w2s_raw")
        plane2 = keep.tile([P, S], U8, name="plane2", align_bytes=64)
        nc.vector.tensor_copy(plane2[:].bitcast(I32), w2s_raw[:].bitcast(I32))
        place_rows(plane2, nc.sync)
        w2 = gather(dw_win[:].bitcast(U32), k2_t, U32, "w2")

        h = [keep.tile([P, S], F32, name="h%d" % t) for t in range(PACK)]
        hg = [keep.tile([P, S], F32, name="hg%d" % t) for t in range(PACK)]

        def leave_psum(t):
            nc.scalar.activation(h[t][:], h_ps[t][:], ACT.Copy, scale=SIXTEENTH)
            nc.vector.tensor_scalar(hg[t][:], h[t][:], gain[:, t : t + 1], None, MULT)

        starts = [sum(CHUNKS[:c]) for c in range(len(CHUNKS))]
        z = [keep.tile([P, PACK, w], F32, name="z%d" % c, tag="z%d" % c) for c, w in enumerate(CHUNKS)]
        zb = [keep.tile([P, w, PACK], BF16, name="zb%d" % c, align_bytes=64) for c, w in enumerate(CHUNKS)]

        sg_ring = [keep.tile([P, max(CHUNKS)], F32, name="sg%d" % i) for i in range(RING)]

        def gate(c, t):
            w = CHUNKS[c]
            lc = slice(starts[c] // 16, (starts[c] + w) // 16)
            sg = sg_ring[(PACK * c + t) % RING][:, 0:w]
            nc.scalar.activation(sg, h[t][:].indirect(n2_t[:, lc]), ACT.Sigmoid)
            nc.vector.tensor_tensor(z[c][:, t, :], hg[t][:].indirect(n1_t[:, lc]), sg, MULT)

        def weave(c):
            dst = zb[c][:].rearrange("p (g i) t -> p g t i", i=4)
            src = z[c][:].rearrange("p t (g i) -> p g t i", i=4)
            if c == WEAVE_ON_SCALAR:
                nc.scalar.copy(dst, src)
            else:
                nc.vector.tensor_copy(dst, src)

        out_v = out.rearrange("(m p) j -> p m j", p=P)

        banks = {}

        def multiply(c):
            w = CHUNKS[c]
            zq = keep.tile([P, w], U32, name="zq%d" % c, align_bytes=64)
            zs = keep.tile([P, w], U8, name="zs%d" % c, align_bytes=64)
            nc.vector.quantize_mx(out=zq[:].bitcast(FP8X4), scales=zs[:], in_=zb[c][:].rearrange("p j t -> p (j t)"))
            last = c == len(CHUNKS) - 1
            per_bank = 2 if last else S // w
            for m0 in range(0, PACK, per_bank):
                o_ps = psum.tile([P, per_bank, w], F32, name="o_ps", tag="o_ps", bufs=4)
                for m in range(m0, m0 + per_bank):
                    cols = slice(m * P, (m + 1) * P)
                    nc.tensor.matmul_mx(
                        out=o_ps[:, m - m0, :], lhsT=w2[:, cols].bitcast(FP8X4), lhsT_scale=plane2[:, cols],
                        rhs=zq[:].bitcast(FP8X4), rhs_scale=zs[:], start=True, stop=True,
                    )
                banks[(c, m0)] = o_ps

        def leave(c):
            w = CHUNKS[c]
            last = c == len(CHUNKS) - 1
            per_bank = 2 if last else S // w
            for m0 in range(0, PACK, per_bank):
                o_ps = banks[(c, m0)]
                tag = "z1" if (c, m0) == (0, 0) else "o_sb%d_%d" % (c, m0)
                o_sb = keep.tile([P, per_bank, w], F32, name="o_sb%d_%d" % (c, m0), tag=tag)
                if last and m0 > 0:
                    nc.vector.tensor_scalar(o_sb[:], o_ps[:], SIXTEENTH, None, MULT)
                else:
                    nc.scalar.activation(o_sb[:], o_ps[:], ACT.Copy, scale=SIXTEENTH)
                nc.sync.dma_start(out_v[:, m0 : m0 + per_bank, starts[c] : starts[c] + w], o_sb[:])

        for t in range(PACK):
            leave_psum(t)
            gate(0, t)
        gate(1, 0)
        weave(0)
        gate(1, 1)
        multiply(0)
        gate(1, 2)
        gate(1, 3)
        weave(1)
        leave(0)
        gate(2, 0)
        gate(2, 1)
        multiply(1)
        leave(1)
        gate(2, 2)
        gate(2, 3)
        weave(2)
        multiply(2)
        leave(2)
